import numpy as np
import ml_dtypes


def mxq(x, axis, fmt="e4m3"):
    dtype, down = {"e4m3": (ml_dtypes.float8_e4m3fn, 7), "e5m2": (ml_dtypes.float8_e5m2, 14)}[fmt]
    v = np.moveaxis(np.asarray(x, np.float32).astype(ml_dtypes.bfloat16).astype(np.float64), axis, -1)
    blocks = v.reshape(v.shape[:-1] + (-1, 32))
    amax = np.abs(blocks).max(-1, keepdims=True)
    byte = np.maximum(np.where(amax > 0, np.frexp(amax)[1] - 1 + 127, 0) - down, 1)
    scale = np.exp2(byte - 127.0)
    codes = (blocks / scale).astype(np.float32).astype(dtype).astype(np.float64)
    return np.moveaxis((codes * scale).reshape(v.shape), -1, axis)


WIDE = False


def mx_kscale(k):
    if not WIDE:
        return np.ones(k)
    levels = np.array([10, -10, 5, -5, 0])
    if k % 512:
        return np.exp2(np.random.permutation(np.resize(levels, k // 32))).repeat(32)
    a = np.empty((k // 512, 16))
    for p in range(k // 512):
        a[p, :8] = np.random.permutation(np.resize(levels, 8))
        for g in range(8):
            far = levels[np.abs(levels - a[p, g]) >= 10]
            a[p, g + 8] = far[np.random.randint(len(far))]
    return np.exp2(a.ravel()).repeat(32)


def f64(x):
    return np.asarray(x).astype(np.float64)


def striped(idx):
    return np.tile(idx.reshape(-1, 16).T, (8, 1)).astype(np.uint16)


def unstriped(offs):
    return offs[:16].T.reshape(-1).astype(np.int64)


def pack_weight(w):
    k, n = w.shape
    w = f64(np.asarray(w, np.float32).astype(ml_dtypes.bfloat16)).reshape(k // 32, 32, n)
    amax = np.abs(w).max(1)
    byte = np.clip(np.where(amax > 0, np.frexp(amax)[1] - 1 + 127 - 7, 1), 1, 254)
    scaled = (w * np.exp2(127.0 - byte)[:, None, :]).reshape(k, n).astype(np.float32)
    words = np.ascontiguousarray(scaled.reshape(k // 512, 128, 4, n).transpose(0, 1, 3, 2)).astype(ml_dtypes.float8_e4m3fn).view(np.uint8)
    return words, np.ascontiguousarray(byte.astype(np.uint8).reshape(k // 512, 16, n))


def unpack_weight(words, scales):
    g, p, n, _ = words.shape
    vals = np.ascontiguousarray(words).view(ml_dtypes.float8_e4m3fn).astype(np.float64) * np.repeat(np.exp2(scales.astype(np.float64) - 127.0), 8, axis=1)[..., None]
    return vals.transpose(0, 1, 3, 2).reshape(g * 512, n)


def relu(v):
    return np.maximum(v, 0.0)


K, T, D, S, V, N = 1024, 512, 8, 2048, 256, 512


def setup_inputs():
    n = np.random.standard_normal
    s = mx_kscale(K)[:, None]
    words, scales = pack_weight(n((K, N)) / np.sqrt(K) / s)
    return {
        "xT": (n((K, T)) * s).astype(np.float32),
        "w_words": words,
        "w_scales": scales,
        "b": (0.3 * n((N, 1))).astype(np.float32),
        "offs": striped(np.concatenate([np.random.permutation(T)[:V] for _ in range(D)])),
    }


def reference(xT, w_words, w_scales, b, offs):
    w = unpack_weight(w_words, w_scales)
    idx = unstriped(offs)
    x = np.empty((K, V))
    for l in range(D):
        r = l // 4 * (4 * K // D) + l % 4 + 4 * np.arange(K // D)
        x[r] = f64(xT)[r][:, idx[l * V:(l + 1) * V]]
    xq = mxq(x, 0, "e4m3")
    return relu((w.T @ xq) + f64(b))

@@ -1,0 +1,118 @@
+from contextlib import ExitStack
+
+import concourse.mybir as mybir
+from concourse.masks import make_identity
+
+F32 = mybir.dt.float32
+BF16 = mybir.dt.bfloat16
+I32 = mybir.dt.int32
+U32 = mybir.dt.uint32
+U16 = mybir.dt.uint16
+U8 = mybir.dt.uint8
+FP8X4 = mybir.dt.float8_e4m3fn_x4
+COPY = mybir.ActivationFunctionType.Copy
+RELU = mybir.ActivationFunctionType.Relu
+ADD = mybir.AluOpType.add
+MAX = mybir.AluOpType.max
+
+P = 128
+T = 512
+V = 256
+N = 512
+PASSES = 2
+PACK = 4
+M_TILES = N // P
+FLOPS = 2 * PASSES * P * PACK * N * V
+
+
+def tile_picked_grid_lin_relu_sub_l_kernel(tc, xT, w_words, w_scales, b, offs, out):
+    nc = tc.nc
+    with ExitStack() as ctx:
+        keep = ctx.enter_context(tc.tile_pool(name="keep", bufs=1))
+        psum = ctx.enter_context(tc.psum_pool(name="psum", bufs=1))
+
+        lists = keep.tile([P, PASSES * PACK * V // 16], U16, name="lists")
+        tables = [keep.tile([P, T], F32, name=f"table{l}") for l in range(PASSES * PACK)]
+        w_codes = [keep.tile([P, N], U32, name=f"w_codes{a}", align_bytes=64) for a in range(PASSES)]
+        w_bytes = keep.tile([P, N], U8, name="w_bytes", align_bytes=64)
+        x_rows = [keep.tile([P, V, PACK], BF16, name=f"x_rows{a}", align_bytes=64) for a in range(PASSES)]
+        x_codes = [keep.tile([P, V], U32, name=f"x_codes{a}", align_bytes=64) for a in range(PASSES)]
+        x_bytes = [keep.tile([P, V], U8, name=f"x_bytes{a}", align_bytes=64) for a in range(PASSES)]
+        warm = keep.tile([P, 8], F32, name="warm")
+        warm_out = keep.tile([P, 8], F32, name="warm_out")
+        ident = keep.tile([P, P], F32, name="ident")
+        b_rows = keep.tile([P, P], F32, name="b_rows")
+        b_cols = keep.tile([P, M_TILES], F32, name="b_cols")
+
+        levels = xT.rearrange("(a f r) w -> a r f w", a=PASSES, r=PACK)
+
+        nc.sync.dma_start(out=lists[:], in_=offs)
+        for l in (2, 0, 3, 1, 4, 5, 6, 7):
+            nc.sync.dma_start(out=tables[l][:], in_=levels[l // PACK, l % PACK])
+        for a in range(PASSES):
+            nc.sync.dma_start(out=w_codes[a][:].bitcast(I32), in_=w_words[a].rearrange("p n r -> p (n r)").bitcast(I32))
+
+        nc.vector.memset(warm[:], 0.0)
+        nc.scalar.activation(warm_out[:], warm[:], COPY)
+        nc.gpsimd.memset(w_bytes[:].bitcast(U32), 0)
+        nc.gpsimd.memset(b_rows[:], 0.0)
+        make_identity(nc, ident[:])
+        nc.gpsimd.dma_start(out=b_rows[0:M_TILES, :], in_=b.rearrange("(c p) o -> c (p o)", p=P))
+        for q in range(4):
+            nc.gpsimd.dma_start(out=w_bytes[32 * q : 32 * q + 8, :].bitcast(I32), in_=w_scales[:, 4 * q : 4 * q + 4, :].bitcast(I32))
+        turned = psum.tile([P, P], F32, name="turned")
+        nc.tensor.transpose(turned[:], b_rows[:], ident[:])
+
+        def piece(l):
+            return lists[:, l * V // 16 : (l + 1) * V // 16]
+
+        def picked(l, table):
+            return table[:].indirect(piece(l))
+
+        accs = [psum.tile([P, V], F32, name=f"acc{c}") for c in range(M_TILES)]
+
+        def quantise(a):
+            nc.vector.quantize_mx(out=x_codes[a][:].bitcast(FP8X4), scales=x_bytes[a][:], in_=x_rows[a][:].rearrange("p v r -> p (v r)"))
+
+        def multiply(a):
+            for c in range(M_TILES):
+                cols = slice(c * P, (c + 1) * P)
+                nc.tensor.matmul_mx(
+                    out=accs[c][:],
+                    lhsT=w_codes[a][:, cols].bitcast(FP8X4),
+                    lhsT_scale=w_bytes[4 * a :, cols],
+                    rhs=x_codes[a][:].bitcast(FP8X4),
+                    rhs_scale=x_bytes[a][:],
+                    start=(a == 0),
+                    stop=(a == PASSES - 1),
+                )
+
+        def pair_by_vector_and_scalar(l):
+            two = keep.tile([P, 2, V], F32, name=f"two{l}")
+            for i in range(2):
+                nc.vector.tensor_copy(two[:, i, :], picked(l + i, tables[l + i]))
+            r = l % PACK
+            nc.scalar.copy(x_rows[l // PACK][:, :, r : r + 2], two[:].rearrange("p i v -> p v i"))
+
+        for l in (0, 1):
+            half = keep.tile([P, T], BF16, name=f"half{l}")
+            nc.scalar.copy(half[:], tables[l][:])
+            nc.scalar.activation(x_rows[0][:, :, l], picked(l, half), COPY)
+        pair_by_vector_and_scalar(2)
+        pair_by_vector_and_scalar(4)
+        quantise(0)
+        multiply(0)
+        nc.scalar.copy(b_cols[:], turned[:, 0:M_TILES])
+        for l in (6, 7):
+            nc.vector.tensor_copy(x_rows[1][:, :, l % PACK], picked(l, tables[l]))
+        quantise(1)
+        multiply(1)
+
+        for c in range(M_TILES):
+            result = keep.tile([P, V], F32, name=f"result{c}")
+            if c % 2 == 0:
+                nc.scalar.activation(result[:], accs[c][:], RELU, bias=b_cols[:, c : c + 1])
+                nc.scalar.dma_start(out=out[c * P : (c + 1) * P, :], in_=result[:])
+            else:
+                nc.vector.tensor_scalar(result[:], accs[c][:], b_cols[:, c : c + 1], 0.0, ADD, MAX)
+                nc.sync.dma_start(out=out[c * P : (c + 1) * P, :], in_=result[:])

@@ -14,6 +14,7 @@ COPY = mybir.ActivationFunctionType.Copy
 RELU = mybir.ActivationFunctionType.Relu
 ADD = mybir.AluOpType.add
 MAX = mybir.AluOpType.max
+MULT = mybir.AluOpType.mult
 
 P = 128
 T = 512
@@ -46,46 +47,68 @@ def tile_picked_grid_lin_relu_sub_l_kernel(tc, xT, w_words, w_scales, b, offs, o
 
         levels = xT.rearrange("(a f r) w -> a r f w", a=PASSES, r=PACK)
 
-        nc.sync.dma_start(out=lists[:], in_=offs)
-        for l in (2, 0, 3, 1, 4, 5, 6, 7):
+        nc.vector.memset(b_rows[:], 0.0)
+        nc.vector.memset(w_bytes[:].bitcast(U32), 0)
+        nc.vector.memset(ident[:], 0.0)
+        nc.vector.memset(warm[:], 0.0)
+        def load_scales(queue, q):
+            queue.dma_start(out=w_bytes[32 * q : 32 * q + 8, :].bitcast(I32), in_=w_scales[:, 4 * q : 4 * q + 4, :].bitcast(I32))
+
+        def load_level(l):
             nc.sync.dma_start(out=tables[l][:], in_=levels[l // PACK, l % PACK])
-        for a in range(PASSES):
+
+        def load_w(a):
             nc.sync.dma_start(out=w_codes[a][:].bitcast(I32), in_=w_words[a].rearrange("p n r -> p (n r)").bitcast(I32))
 
-        nc.vector.memset(warm[:], 0.0)
+        nc.sync.dma_start(out=lists[:], in_=offs)
+        for l in (0, 1, 4, 2, 5):
+            load_level(l)
+        load_scales(nc.scalar, 0)
+        load_scales(nc.scalar, 1)
+        load_level(3)
+        load_level(6)
+        load_w(0)
+        load_level(7)
+        load_w(1)
         nc.scalar.activation(warm_out[:], warm[:], COPY)
-        nc.gpsimd.memset(w_bytes[:].bitcast(U32), 0)
-        nc.gpsimd.memset(b_rows[:], 0.0)
-        make_identity(nc, ident[:])
+        make_identity(nc, ident[:], nomemset=True)
+        load_scales(nc.gpsimd, 2)
+        load_scales(nc.gpsimd, 3)
         nc.gpsimd.dma_start(out=b_rows[0:M_TILES, :], in_=b.rearrange("(c p) o -> c (p o)", p=P))
-        for q in range(4):
-            nc.gpsimd.dma_start(out=w_bytes[32 * q : 32 * q + 8, :].bitcast(I32), in_=w_scales[:, 4 * q : 4 * q + 4, :].bitcast(I32))
         turned = psum.tile([P, P], F32, name="turned")
         nc.tensor.transpose(turned[:], b_rows[:], ident[:])
 
-        def piece(l):
-            return lists[:, l * V // 16 : (l + 1) * V // 16]
-
-        def picked(l, table):
-            return table[:].indirect(piece(l))
+        def picked(l, table, v0=0, v1=V):
+            return table[:].indirect(lists[:, (l * V + v0) // 16 : (l * V + v1) // 16])
 
         accs = [psum.tile([P, V], F32, name=f"acc{c}") for c in range(M_TILES)]
 
-        def quantise(a):
-            nc.vector.quantize_mx(out=x_codes[a][:].bitcast(FP8X4), scales=x_bytes[a][:], in_=x_rows[a][:].rearrange("p v r -> p (v r)"))
+        def quantise(a, v0=0, v1=V):
+            nc.vector.quantize_mx(
+                out=x_codes[a][:, v0:v1].bitcast(FP8X4),
+                scales=x_bytes[a][:, v0:v1],
+                in_=x_rows[a][:, v0:v1, :].rearrange("p v r -> p (v r)"),
+            )
 
-        def multiply(a):
-            for c in range(M_TILES):
-                cols = slice(c * P, (c + 1) * P)
-                nc.tensor.matmul_mx(
-                    out=accs[c][:],
-                    lhsT=w_codes[a][:, cols].bitcast(FP8X4),
-                    lhsT_scale=w_bytes[4 * a :, cols],
-                    rhs=x_codes[a][:].bitcast(FP8X4),
-                    rhs_scale=x_bytes[a][:],
-                    start=(a == 0),
-                    stop=(a == PASSES - 1),
-                )
+        def multiply(a, c, v0=0, v1=V):
+            cols = slice(c * P, (c + 1) * P)
+            nc.tensor.matmul_mx(
+                out=accs[c][:, v0:v1],
+                lhsT=w_codes[a][:, cols].bitcast(FP8X4),
+                lhsT_scale=w_bytes[4 * a :, cols],
+                rhs=x_codes[a][:, v0:v1].bitcast(FP8X4),
+                rhs_scale=x_bytes[a][:, v0:v1],
+                start=(a == 0),
+                stop=(a == PASSES - 1 and v1 == V),
+            )
+
+        def by_scalar(l):
+            half = keep.tile([P, T], BF16, name=f"half{l}")
+            nc.vector.tensor_copy(half[:], tables[l][:])
+            nc.scalar.activation(x_rows[l // PACK][:, :, l % PACK], picked(l, half), COPY)
+
+        def by_vector(l, v0=0, v1=V):
+            nc.vector.tensor_copy(x_rows[l // PACK][:, v0:v1, l % PACK], picked(l, tables[l], v0, v1))
 
         def pair_by_vector_and_scalar(l):
             two = keep.tile([P, 2, V], F32, name=f"two{l}")
@@ -94,19 +117,25 @@ def tile_picked_grid_lin_relu_sub_l_kernel(tc, xT, w_words, w_scales, b, offs, o
             r = l % PACK
             nc.scalar.copy(x_rows[l // PACK][:, :, r : r + 2], two[:].rearrange("p i v -> p v i"))
 
-        for l in (0, 1):
-            half = keep.tile([P, T], BF16, name=f"half{l}")
-            nc.scalar.copy(half[:], tables[l][:])
-            nc.scalar.activation(x_rows[0][:, :, l], picked(l, half), COPY)
-        pair_by_vector_and_scalar(2)
-        pair_by_vector_and_scalar(4)
+        H = V // 2
+        by_scalar(0)
+        by_scalar(1)
+        by_vector(4)
+        by_scalar(2)
+        by_vector(5)
+        by_scalar(3)
+        by_vector(6)
         quantise(0)
-        multiply(0)
+        for c in range(M_TILES):
+            multiply(0, c)
+        by_vector(7, 0, H)
+        by_vector(7, H, V)
+        quantise(1, 0, H)
+        quantise(1, H, V)
         nc.scalar.copy(b_cols[:], turned[:, 0:M_TILES])
-        for l in (6, 7):
-            nc.vector.tensor_copy(x_rows[1][:, :, l % PACK], picked(l, tables[l]))
-        quantise(1)
-        multiply(1)
+        for v0 in (0, H):
+            for c in range(M_TILES):
+                multiply(1, c, v0, v0 + H)
 
         for c in range(M_TILES):
             result = keep.tile([P, V], F32, name=f"result{c}")

@@ -60,8 +60,9 @@ def tile_picked_grid_lin_relu_sub_l_kernel(tc, xT, w_words, w_scales, b, offs, o
         def load_w(a):
             nc.sync.dma_start(out=w_codes[a][:].bitcast(I32), in_=w_words[a].rearrange("p n r -> p (n r)").bitcast(I32))
 
+        load_level(0)
         nc.sync.dma_start(out=lists[:], in_=offs)
-        for l in (0, 1, 4, 2, 5):
+        for l in (1, 4, 2, 5):
             load_level(l)
         load_scales(nc.scalar, 0)
         load_scales(nc.scalar, 1)
@@ -75,13 +76,14 @@ def tile_picked_grid_lin_relu_sub_l_kernel(tc, xT, w_words, w_scales, b, offs, o
         load_scales(nc.gpsimd, 2)
         load_scales(nc.gpsimd, 3)
         nc.gpsimd.dma_start(out=b_rows[0:M_TILES, :], in_=b.rearrange("(c p) o -> c (p o)", p=P))
-        turned = psum.tile([P, P], F32, name="turned")
+        turned = psum.tile([P, P], F32, name="turned", tag="acc3_1")
         nc.tensor.transpose(turned[:], b_rows[:], ident[:])
 
         def picked(l, table, v0=0, v1=V):
             return table[:].indirect(lists[:, (l * V + v0) // 16 : (l * V + v1) // 16])
 
-        accs = [psum.tile([P, V], F32, name=f"acc{c}") for c in range(M_TILES)]
+        H = V // 2
+        accs = [[psum.tile([P, H], F32, name=f"acc{c}_{h}", tag=f"acc{c}_{h}") for h in range(2)] for c in range(M_TILES)]
 
         def quantise(a, v0=0, v1=V):
             nc.vector.quantize_mx(
@@ -90,16 +92,17 @@ def tile_picked_grid_lin_relu_sub_l_kernel(tc, xT, w_words, w_scales, b, offs, o
                 in_=x_rows[a][:, v0:v1, :].rearrange("p v r -> p (v r)"),
             )
 
-        def multiply(a, c, v0=0, v1=V):
+        def multiply(a, c, h):
             cols = slice(c * P, (c + 1) * P)
+            points = slice(h * H, (h + 1) * H)
             nc.tensor.matmul_mx(
-                out=accs[c][:, v0:v1],
+                out=accs[c][h][:],
                 lhsT=w_codes[a][:, cols].bitcast(FP8X4),
                 lhsT_scale=w_bytes[4 * a :, cols],
-                rhs=x_codes[a][:, v0:v1].bitcast(FP8X4),
-                rhs_scale=x_bytes[a][:, v0:v1],
+                rhs=x_codes[a][:, points].bitcast(FP8X4),
+                rhs_scale=x_bytes[a][:, points],
                 start=(a == 0),
-                stop=(a == PASSES - 1 and v1 == V),
+                stop=(a == PASSES - 1),
             )
 
         def by_scalar(l):
@@ -110,38 +113,32 @@ def tile_picked_grid_lin_relu_sub_l_kernel(tc, xT, w_words, w_scales, b, offs, o
         def by_vector(l, v0=0, v1=V):
             nc.vector.tensor_copy(x_rows[l // PACK][:, v0:v1, l % PACK], picked(l, tables[l], v0, v1))
 
-        def pair_by_vector_and_scalar(l):
-            two = keep.tile([P, 2, V], F32, name=f"two{l}")
-            for i in range(2):
-                nc.vector.tensor_copy(two[:, i, :], picked(l + i, tables[l + i]))
-            r = l % PACK
-            nc.scalar.copy(x_rows[l // PACK][:, :, r : r + 2], two[:].rearrange("p i v -> p v i"))
-
-        H = V // 2
         by_scalar(0)
         by_scalar(1)
         by_vector(4)
         by_scalar(2)
         by_vector(5)
         by_scalar(3)
+        nc.scalar.copy(b_cols[:], turned[:, 0:M_TILES])
         by_vector(6)
         quantise(0)
-        for c in range(M_TILES):
-            multiply(0, c)
+        for h in range(2):
+            for c in range(M_TILES):
+                multiply(0, c, h)
         by_vector(7, 0, H)
         by_vector(7, H, V)
         quantise(1, 0, H)
         quantise(1, H, V)
-        nc.scalar.copy(b_cols[:], turned[:, 0:M_TILES])
-        for v0 in (0, H):
+        results = [keep.tile([P, V], F32, name=f"result{c}") for c in range(M_TILES)]
+        for h in range(2):
             for c in range(M_TILES):
-                multiply(1, c, v0, v0 + H)
-
+                multiply(1, c, h)
+            for c in range(M_TILES):
+                part = results[c][:, h * H : (h + 1) * H]
+                if c % 2 == 0:
+                    nc.scalar.activation(part, accs[c][h][:], RELU, bias=b_cols[:, c : c + 1])
+                else:
+                    nc.vector.tensor_scalar(part, accs[c][h][:], b_cols[:, c : c + 1], 0.0, ADD, MAX)
         for c in range(M_TILES):
-            result = keep.tile([P, V], F32, name=f"result{c}")
-            if c % 2 == 0:
-                nc.scalar.activation(result[:], accs[c][:], RELU, bias=b_cols[:, c : c + 1])
-                nc.scalar.dma_start(out=out[c * P : (c + 1) * P, :], in_=result[:])
-            else:
-                nc.vector.tensor_scalar(result[:], accs[c][:], b_cols[:, c : c + 1], 0.0, ADD, MAX)
-                nc.sync.dma_start(out=out[c * P : (c + 1) * P, :], in_=result[:])
+            queue = nc.scalar if c % 2 == 0 else nc.sync
+            queue.dma_start(out=out[c * P : (c + 1) * P, :], in_=results[c][:])

from contextlib import ExitStack

import concourse.mybir as mybir
from concourse.masks import make_identity

F32 = mybir.dt.float32
BF16 = mybir.dt.bfloat16
I32 = mybir.dt.int32
U32 = mybir.dt.uint32
U16 = mybir.dt.uint16
U8 = mybir.dt.uint8
FP8X4 = mybir.dt.float8_e4m3fn_x4
COPY = mybir.ActivationFunctionType.Copy
RELU = mybir.ActivationFunctionType.Relu
ADD = mybir.AluOpType.add
MAX = mybir.AluOpType.max
MULT = mybir.AluOpType.mult

P = 128
T = 512
V = 256
N = 512
PASSES = 2
PACK = 4
M_TILES = N // P
FLOPS = 2 * PASSES * P * PACK * N * V


def tile_picked_grid_lin_relu_sub_l_kernel(tc, xT, w_words, w_scales, b, offs, out):
    nc = tc.nc
    with ExitStack() as ctx:
        keep = ctx.enter_context(tc.tile_pool(name="keep", bufs=1))
        psum = ctx.enter_context(tc.psum_pool(name="psum", bufs=1))

        lists = keep.tile([P, PASSES * PACK * V // 16], U16, name="lists")
        tables = [keep.tile([P, T], F32, name=f"table{l}") for l in range(PASSES * PACK)]
        w_codes = [keep.tile([P, N], U32, name=f"w_codes{a}", align_bytes=64) for a in range(PASSES)]
        w_bytes = keep.tile([P, N], U8, name="w_bytes", align_bytes=64)
        x_rows = [keep.tile([P, V, PACK], BF16, name=f"x_rows{a}", align_bytes=64) for a in range(PASSES)]
        x_codes = [keep.tile([P, V], U32, name=f"x_codes{a}", align_bytes=64) for a in range(PASSES)]
        x_bytes = [keep.tile([P, V], U8, name=f"x_bytes{a}", align_bytes=64) for a in range(PASSES)]
        warm = keep.tile([P, 8], F32, name="warm")
        warm_out = keep.tile([P, 8], F32, name="warm_out")
        ident = keep.tile([P, P], F32, name="ident")
        b_rows = keep.tile([P, P], F32, name="b_rows")
        b_cols = keep.tile([P, M_TILES], F32, name="b_cols")

        levels = xT.rearrange("(a f r) w -> a r f w", a=PASSES, r=PACK)

        nc.vector.memset(b_rows[:], 0.0)
        nc.vector.memset(w_bytes[:].bitcast(U32), 0)
        nc.vector.memset(ident[:], 0.0)
        nc.vector.memset(warm[:], 0.0)
        def load_scales(queue, q):
            queue.dma_start(out=w_bytes[32 * q : 32 * q + 8, :].bitcast(I32), in_=w_scales[:, 4 * q : 4 * q + 4, :].bitcast(I32))

        def load_level(l):
            nc.sync.dma_start(out=tables[l][:], in_=levels[l // PACK, l % PACK])

        def load_w(a):
            nc.sync.dma_start(out=w_codes[a][:].bitcast(I32), in_=w_words[a].rearrange("p n r -> p (n r)").bitcast(I32))

        load_level(0)
        nc.sync.dma_start(out=lists[:], in_=offs)
        for l in (1, 4, 2, 5):
            load_level(l)
        load_scales(nc.scalar, 0)
        load_scales(nc.scalar, 1)
        load_level(3)
        load_level(6)
        load_w(0)
        load_level(7)
        load_w(1)
        nc.scalar.activation(warm_out[:], warm[:], COPY)
        make_identity(nc, ident[:], nomemset=True)
        load_scales(nc.gpsimd, 2)
        load_scales(nc.gpsimd, 3)
        nc.gpsimd.dma_start(out=b_rows[0:M_TILES, :], in_=b.rearrange("(c p) o -> c (p o)", p=P))
        turned = psum.tile([P, P], F32, name="turned", tag="acc3_1")
        nc.tensor.transpose(turned[:], b_rows[:], ident[:])

        def picked(l, table, v0=0, v1=V):
            return table[:].indirect(lists[:, (l * V + v0) // 16 : (l * V + v1) // 16])

        H = V // 2
        accs = [[psum.tile([P, H], F32, name=f"acc{c}_{h}", tag=f"acc{c}_{h}") for h in range(2)] for c in range(M_TILES)]

        def quantise(a, v0=0, v1=V):
            nc.vector.quantize_mx(
                out=x_codes[a][:, v0:v1].bitcast(FP8X4),
                scales=x_bytes[a][:, v0:v1],
                in_=x_rows[a][:, v0:v1, :].rearrange("p v r -> p (v r)"),
            )

        def multiply(a, c, h):
            cols = slice(c * P, (c + 1) * P)
            points = slice(h * H, (h + 1) * H)
            nc.tensor.matmul_mx(
                out=accs[c][h][:],
                lhsT=w_codes[a][:, cols].bitcast(FP8X4),
                lhsT_scale=w_bytes[4 * a :, cols],
                rhs=x_codes[a][:, points].bitcast(FP8X4),
                rhs_scale=x_bytes[a][:, points],
                start=(a == 0),
                stop=(a == PASSES - 1),
            )

        def by_scalar(l):
            half = keep.tile([P, T], BF16, name=f"half{l}")
            nc.vector.tensor_copy(half[:], tables[l][:])
            nc.scalar.activation(x_rows[l // PACK][:, :, l % PACK], picked(l, half), COPY)

        def by_vector(l, v0=0, v1=V):
            nc.vector.tensor_copy(x_rows[l // PACK][:, v0:v1, l % PACK], picked(l, tables[l], v0, v1))

        by_scalar(0)
        by_scalar(1)
        by_vector(4)
        by_scalar(2)
        by_vector(5)
        by_scalar(3)
        nc.scalar.copy(b_cols[:], turned[:, 0:M_TILES])
        by_vector(6)
        quantise(0)
        for h in range(2):
            for c in range(M_TILES):
                multiply(0, c, h)
        by_vector(7, 0, H)
        by_vector(7, H, V)
        quantise(1, 0, H)
        quantise(1, H, V)
        results = [keep.tile([P, V], F32, name=f"result{c}") for c in range(M_TILES)]
        for h in range(2):
            for c in range(M_TILES):
                multiply(1, c, h)
            for c in range(M_TILES):
                part = results[c][:, h * H : (h + 1) * H]
                if c % 2 == 0:
                    nc.scalar.activation(part, accs[c][h][:], RELU, bias=b_cols[:, c : c + 1])
                else:
                    nc.vector.tensor_scalar(part, accs[c][h][:], b_cols[:, c : c + 1], 0.0, ADD, MAX)
        for c in range(M_TILES):
            queue = nc.scalar if c % 2 == 0 else nc.sync
            queue.dma_start(out=out[c * P : (c + 1) * P, :], in_=results[c][:])
